import numpy as np
import ml_dtypes


def mxq(x, axis, fmt="e4m3"):
    dtype, down = {"e4m3": (ml_dtypes.float8_e4m3fn, 7), "e5m2": (ml_dtypes.float8_e5m2, 14)}[fmt]
    v = np.moveaxis(np.asarray(x, np.float32).astype(ml_dtypes.bfloat16).astype(np.float64), axis, -1)
    blocks = v.reshape(v.shape[:-1] + (-1, 32))
    amax = np.abs(blocks).max(-1, keepdims=True)
    byte = np.maximum(np.where(amax > 0, np.frexp(amax)[1] - 1 + 127, 0) - down, 1)
    scale = np.exp2(byte - 127.0)
    codes = (blocks / scale).astype(np.float32).astype(dtype).astype(np.float64)
    return np.moveaxis((codes * scale).reshape(v.shape), -1, axis)


WIDE = False


def mx_kscale(k):
    if not WIDE:
        return np.ones(k)
    levels = np.array([10, -10, 5, -5, 0])
    if k % 512:
        return np.exp2(np.random.permutation(np.resize(levels, k // 32))).repeat(32)
    a = np.empty((k // 512, 16))
    for p in range(k // 512):
        a[p, :8] = np.random.permutation(np.resize(levels, 8))
        for g in range(8):
            far = levels[np.abs(levels - a[p, g]) >= 10]
            a[p, g + 8] = far[np.random.randint(len(far))]
    return np.exp2(a.ravel()).repeat(32)


BF16 = ml_dtypes.bfloat16


def bf(x):
    return np.asarray(x, np.float32).astype(BF16)


def f64(x):
    return np.asarray(x).astype(np.float64)


E2M1 = np.array([0.0, 0.5, 1.0, 1.5, 2.0, 3.0, 4.0, 6.0, -0.0, -0.5, -1.0, -1.5, -2.0, -3.0, -4.0, -6.0])


def pack_weight(w, fmt):
    k, n = w.shape
    w = f64(bf(w)).reshape(k // 32, 32, n)
    amax = np.abs(w).max(1)
    if fmt == "e4m3":
        byte = np.frexp(amax)[1] - 1 + 127 - 7
    else:
        mant, ex = np.frexp(amax / 6.0)
        byte = np.where(mant > 0.5, ex, ex - 1) + 127
    byte = np.clip(np.where(amax > 0, byte, 1), 1, 254)
    scaled = (w * np.exp2(127.0 - byte)[:, None, :]).reshape(k, n).astype(np.float32)
    by_word = np.ascontiguousarray(scaled.reshape(k // 512, 128, 4, n).transpose(0, 1, 3, 2))
    if fmt == "e4m3":
        words = by_word.astype(ml_dtypes.float8_e4m3fn).view(np.uint8)
    else:
        c = by_word.astype(ml_dtypes.float4_e2m1fn).view(np.uint8) & 0xF
        words = c[..., 0::2] | (c[..., 1::2] << 4)
    return np.ascontiguousarray(words), np.ascontiguousarray(byte.astype(np.uint8).reshape(k // 512, 16, n))


def unpack_weight(words, scales, fmt):
    g, p, n, _ = words.shape
    if fmt == "e4m3":
        vals = np.ascontiguousarray(words).view(ml_dtypes.float8_e4m3fn).astype(np.float64)
    else:
        nib = np.empty((g, p, n, 4), np.uint8)
        nib[..., 0::2] = words & 0xF
        nib[..., 1::2] = words >> 4
        vals = E2M1[nib]
    vals = vals * np.repeat(np.exp2(scales.astype(np.float64) - 127.0), 8, axis=1)[..., None]
    return vals.transpose(0, 1, 3, 2).reshape(g * 512, n)

def planes(Y):
    n, m = Y.shape
    b = f64(bf(Y)).reshape(n // 32, 32, m)
    amax = np.abs(b).max(1)
    byte = np.clip(np.where(amax > 0, np.frexp(amax)[1] - 1 + 127 - 7, 1), 1, 254)
    codes = (b * np.exp2(127.0 - byte)[:, None, :]).reshape(n, m).astype(np.float32).astype(ml_dtypes.float8_e4m3fn).view(np.uint8)
    words = codes.reshape(n // 512, 128, 4, m).transpose(0, 1, 3, 2)
    return np.ascontiguousarray(words), np.ascontiguousarray(byte.astype(np.uint8).reshape(n // 512, 16, m))


N, D, J, V = 1024, 1024, 1024, 1536


def setup_inputs():
    sh, se, t = mx_kscale(D), mx_kscale(D), mx_kscale(J)
    h = bf(np.random.standard_normal((N, D)) * sh)
    emb_words, emb_scales = pack_weight((np.random.standard_normal((V, D)) * se).T, "e4m3")
    u_words, u_scales = pack_weight(np.random.standard_normal((D, J)) / np.sqrt(D) / se[:, None], "e4m3")
    vp_words, vp_scales = pack_weight(np.random.standard_normal((D, J)) / np.sqrt(D) / sh[:, None], "e4m3")
    return {
        "h": h,
        "emb_words": emb_words,
        "emb_scales": emb_scales,
        "u_words": u_words,
        "u_scales": u_scales,
        "vp_words": vp_words,
        "vp_scales": vp_scales,
        "bj": bf(0.3 * np.random.standard_normal((2, J))),
        "gu": bf((1.0 + 0.1 * np.random.standard_normal(J)) / t),
        "gv": bf((1.0 + 0.1 * np.random.standard_normal(J)) * t),
    }


def joint_projection(x, w, b, g):
    y = x @ w
    return np.tanh(y + b[None, :]) * g[None, :]


def core(h, emb_words, emb_scales, u_words, u_scales, vp_words, vp_scales, bj, gu, gv):
    h, bj, gu, gv = f64(h), f64(bj), f64(gu), f64(gv)
    emb = unpack_weight(emb_words, emb_scales, "e4m3").T
    u = unpack_weight(u_words, u_scales, "e4m3")
    vp = unpack_weight(vp_words, vp_scales, "e4m3")
    joint_dim = u.shape[1]
    vocab = emb.shape[0]
    lab = joint_projection(emb, u, bj[0], gu)
    ctx = joint_projection(mxq(h, 1, "e4m3"), vp, bj[1], gv)
    scale = 2.0 / np.sqrt(joint_dim)
    s = scale * (mxq(ctx, 1, "e4m3") @ mxq(lab, 1, "e4m3").T)
    m = s.max(axis=1, keepdims=True)
    lse = m + np.log(np.exp(s - m).sum(axis=1, keepdims=True))
    return s - lse + np.log(vocab)


def reference(h, emb_words, emb_scales, u_words, u_scales, vp_words, vp_scales, bj, gu, gv):
    R_out = core(h, emb_words, emb_scales, u_words, u_scales, vp_words, vp_scales, bj, gu, gv)
    words, scales = planes(R_out.T)
    return R_out, words, scales

@@ -1,0 +1,422 @@
+import math
+from contextlib import ExitStack
+
+import concourse.mybir as mybir
+from concourse.masks import make_identity
+
+F32 = mybir.dt.float32
+BF16 = mybir.dt.bfloat16
+I32 = mybir.dt.int32
+U8 = mybir.dt.uint8
+FP8X4 = mybir.dt.float8_e4m3fn_x4
+ACT = mybir.ActivationFunctionType
+ALU = mybir.AluOpType
+AX = mybir.AxisListType
+
+P = 128
+N, D, J, V = 1024, 1024, 1024, 1536
+KG = 2
+JG = 2
+VG = V // 512
+NT = N // P
+SCALE = 2.0 / math.sqrt(J)
+LN2 = math.log(2.0)
+FLOPS = 2 * (V * D * J + N * D * J + N * J * V)
+
+
+def tile_jointinputoutputembeddingtiedhead_x2_kernel(
+    tc, h, emb_words, emb_scales, u_words, u_scales, vp_words, vp_scales, bj, gu, gv, out, out_words, out_scales
+):
+    nc = tc.nc
+    ctx_stack = ExitStack()
+    with ctx_stack as es:
+        keep = es.enter_context(tc.tile_pool(name="keep", bufs=1))
+        stage = es.enter_context(tc.tile_pool(name="stage", bufs=3))
+        small = es.enter_context(tc.tile_pool(name="small", bufs=8))
+        psum = es.enter_context(tc.psum_pool(name="psum", bufs=6))
+        psum_t = es.enter_context(tc.psum_pool(name="psum_t", bufs=2))
+        es.enter_context(tc.manual_schedule())
+
+        rows = keep.tile([P, 512], BF16, name="rows")
+        nc.gpsimd.memset(rows[:], 0.0)
+        uv_packed = keep.tile([P, J], U8, name="uv_packed", align_bytes=64)
+        nc.vector.memset(uv_packed[:].bitcast(I32), 0)
+        emb_packed = keep.tile([P, V], U8, name="emb_packed", align_bytes=64)
+        nc.vector.memset(emb_packed[:].bitcast(I32), 0)
+
+        nc.scalar.dma_start(out=rows[0:4, :], in_=bj.rearrange("v (g x) -> (v g) x", g=JG))
+        nc.scalar.dma_start(out=rows[4:6, :], in_=gu.rearrange("(g x) -> g x", g=JG))
+        nc.scalar.dma_start(out=rows[6:8, :], in_=gv.rearrange("(g x) -> g x", g=JG))
+
+        for q in range(4):
+            nc.sync.dma_start(out=uv_packed[32 * q : 32 * q + 8, :].bitcast(I32), in_=u_scales[:, 4 * q : 4 * q + 4, :].bitcast(I32))
+            nc.sync.dma_start(out=uv_packed[32 * q + 8 : 32 * q + 16, :].bitcast(I32), in_=vp_scales[:, 4 * q : 4 * q + 4, :].bitcast(I32))
+            nc.sync.dma_start(out=emb_packed[32 * q : 32 * q + 8, :].bitcast(I32), in_=emb_scales[:, 4 * q : 4 * q + 4, :].bitcast(I32))
+
+        u_raw = keep.tile([P, KG, J], I32, name="u_raw", align_bytes=64)
+        vp_raw = keep.tile([P, KG, J], I32, name="vp_raw", align_bytes=64)
+        emb_codes = keep.tile([P, KG, V], I32, name="emb_codes", align_bytes=64)
+        h_raw = [keep.tile([P, D], BF16, name=f"h_raw{i}", align_bytes=64) for i in range(NT)]
+
+        def load_words(tile, words, g, c0, c1):
+            nc.sync.dma_start(out=tile[:, g, c0:c1], in_=words[g].rearrange("p n t -> p (n t)")[:, 4 * c0 : 4 * c1].bitcast(I32))
+
+        def load_h(i):
+            nc.sync.dma_start(out=h_raw[i][:], in_=h[P * i : P * (i + 1), :])
+
+        for g in range(KG):
+            load_words(u_raw, u_words, g, 0, 512)
+        for c0, c1 in ((0, 256), (256, 512), (512, 1024)):
+            for g in range(KG):
+                load_words(emb_codes, emb_words, g, c0, c1)
+        for g in range(KG):
+            load_words(u_raw, u_words, g, 512, 1024)
+        for g in range(KG):
+            load_words(vp_raw, vp_words, g, 0, 1024)
+        for i in range(4):
+            load_h(i)
+        for g in range(KG):
+            load_words(emb_codes, emb_words, g, 1024, 1536)
+        for i in range(4, 8):
+            load_h(i)
+
+        expo = keep.tile([P, 2], F32, name="expo")
+        nc.gpsimd.memset(expo[:, 0:1], 1.0 / 64.0)
+        nc.gpsimd.memset(expo[:, 1:2], -1.0 / 64.0)
+        ident = keep.tile([P, P], F32, name="ident")
+        make_identity(nc, ident[:])
+
+        rows_p = keep.tile([P, 512], F32, name="rows_p")
+        nc.vector.tensor_copy(
+            out=rows_p[:].rearrange("p (t b i) -> p t b i", t=4, i=8),
+            in_=rows[:].rearrange("p (b t i) -> p t b i", t=4, i=8),
+        )
+        cols_ps = psum_t.tile([P, 4, P], F32, name="cols_ps", tag="tp")
+        for t in range(4):
+            nc.tensor.transpose(cols_ps[:, t, :], rows_p[:, P * t : P * (t + 1)], ident[:])
+        cols = keep.tile([P, 8, 4], F32, name="cols")
+        nc.scalar.copy(out=cols[:], in_=cols_ps[:, :, 0:8].rearrange("p t r -> p r t"))
+
+        uv_scales = keep.tile([P, JG, 4, P], U8, name="uv_scales", align_bytes=64)
+        u_codes = keep.tile([P, KG, JG, 4, P], I32, name="u_codes", align_bytes=64)
+        vp_codes = keep.tile([P, KG, JG, 4, P], I32, name="vp_codes", align_bytes=64)
+
+        def permute(dst, source):
+            nc.vector.tensor_copy(
+                out=dst.rearrange("p t (b i) -> p t b i", i=8),
+                in_=source.rearrange("p (b t i) -> p t b i", t=4, i=8),
+            )
+
+        def permute_words(dst, raw, gj):
+            for g in range(KG):
+                permute(dst[:, g, gj], raw[:, g, 512 * gj : 512 * (gj + 1)])
+
+        def permute_scales(gj):
+            permute(uv_scales[:, gj], uv_packed[:, 512 * gj : 512 * (gj + 1)])
+
+        lab_codes = keep.tile([P, JG, V], I32, name="lab_codes", align_bytes=64)
+        lab_scales = keep.tile([P, JG, V], U8, name="lab_scales", align_bytes=64)
+        h_codes = keep.tile([P, KG, N], I32, name="h_codes", align_bytes=64)
+        h_scales = keep.tile([P, KG, N], U8, name="h_scales", align_bytes=64)
+        ctx_codes = keep.tile([P, JG, N], I32, name="ctx_codes", align_bytes=64)
+        ctx_scales = keep.tile([P, JG, N], U8, name="ctx_scales", align_bytes=64)
+        plane_scales = keep.tile([P, VG, N], U8, name="plane_scales", align_bytes=64)
+
+        th_t = {}
+        gained_t = {}
+
+        def label_unit(c0, w, gj):
+            return ("lab", c0, w, gj)
+
+        def context_unit(c0, w, gj):
+            return ("ctx", c0, w, gj)
+
+        def project(unit):
+            kind, c0, w, gj = unit
+            codes_w, plane0, bias_row = (u_codes, 0, 0) if kind == "lab" else (vp_codes, 8, 2)
+            th = stage.tile([P, 4, w], F32, name="th", tag="th", bufs=3)
+            th_t[unit] = th
+            for t in range(4):
+                acc = psum.tile([P, w], F32, name="acc", tag="acc")
+                for g in range(KG):
+                    if kind == "lab":
+                        rhs, rhs_scale = emb_codes[:, g, c0 : c0 + w], emb_packed[4 * g :, c0 : c0 + w]
+                    else:
+                        rhs, rhs_scale = h_codes[:, g, c0 : c0 + w], h_scales[:, g, c0 : c0 + w]
+                    nc.tensor.matmul_mx(
+                        out=acc[:],
+                        lhsT=codes_w[:, g, gj, t, :].bitcast(FP8X4),
+                        lhsT_scale=uv_scales[plane0 + 4 * g :, gj, t, :],
+                        rhs=rhs.bitcast(FP8X4),
+                        rhs_scale=rhs_scale,
+                        start=(g == 0),
+                        stop=(g == KG - 1),
+                    )
+                nc.scalar.activation(out=th[:, t, :], in_=acc[:], func=ACT.Tanh, bias=cols[:, bias_row + gj, t : t + 1], scale=1.0)
+
+        def gain(unit, part=0, parts=1):
+            kind, c0, w, gj = unit
+            if part == 0:
+                gained_t[unit] = stage.tile([P, w, 4], BF16, name="gained", tag="gained", align_bytes=64)
+            gain_row = 4 if kind == "lab" else 6
+            n = w // parts
+            cs = slice(n * part, n * (part + 1))
+            nc.vector.tensor_tensor(
+                out=gained_t[unit][:, cs, :].rearrange("p (c i) t -> p c t i", i=4),
+                in0=th_t[unit][:, :, cs].rearrange("p t (c i) -> p c t i", i=4),
+                in1=cols[:, gain_row + gj, :].unsqueeze(1).unsqueeze(3).to_broadcast([P, n // 4, 4, 4]),
+                op=ALU.mult,
+            )
+
+        def quant(unit):
+            kind, c0, w, gj = unit
+            codes, scales = (lab_codes, lab_scales) if kind == "lab" else (ctx_codes, ctx_scales)
+            nc.vector.quantize_mx(
+                out=codes[:, gj, c0 : c0 + w].bitcast(FP8X4),
+                scales=scales[:, gj, c0 : c0 + w],
+                in_=gained_t[unit][:].rearrange("p c t -> p (c t)"),
+            )
+
+        h_grouped = {}
+
+        def h_turn(k):
+            if k % 4 == 0:
+                h_grouped[k // 4] = stage.tile([P, KG, 512, 4], BF16, name="h_grouped", tag="h_grouped", bufs=2, align_bytes=64)
+            grouped = h_grouped[k // 4]
+            words = h_raw[k][:].bitcast(F32)
+            xt = psum_t.tile([P, KG, 2, P], F32, name="xt", tag="tp")
+            for g in range(KG):
+                for u in range(2):
+                    nc.tensor.transpose(xt[:, g, u, :], words[:, 256 * g + u : 256 * (g + 1) : 2], ident[:])
+            r0 = P * (k % 4)
+            nc.scalar.copy(
+                out=grouped[:, :, r0 : r0 + P, :].rearrange("p g r t -> p g (r t)").bitcast(F32).rearrange("p g (r u) -> p g r u", u=2),
+                in_=xt[:].rearrange("p g u r -> p g r u"),
+            )
+
+        def h_quant(hh, g):
+            nc.vector.quantize_mx(
+                out=h_codes[:, g, 512 * hh : 512 * (hh + 1)].bitcast(FP8X4),
+                scales=h_scales[:, g, 512 * hh : 512 * (hh + 1)],
+                in_=h_grouped[hh][:, g].rearrange("p r t -> p (r t)"),
+            )
+
+        neg = {}
+        cvals = {}
+        outb = {}
+
+        stats = {}
+
+        def scores(i):
+            n_t = stage.tile([P, V], F32, name="neg", tag="neg", bufs=4)
+            neg[i] = n_t
+            vs = small.tile([P, 8], F32, name="vs", tag="vs")
+            gs = small.tile([P, 16], F32, name="gs", tag="gs")
+            stats[i] = (vs, gs)
+            for c in range(VG):
+                acc = psum.tile([P, 512], F32, name="accs", tag="acc")
+                for g in range(JG):
+                    nc.tensor.matmul_mx(
+                        out=acc[:],
+                        lhsT=ctx_codes[:, g, P * i : P * (i + 1)].bitcast(FP8X4),
+                        lhsT_scale=ctx_scales[:, g, P * i : P * (i + 1)],
+                        rhs=lab_codes[:, g, 512 * c : 512 * (c + 1)].bitcast(FP8X4),
+                        rhs_scale=lab_scales[:, g, 512 * c : 512 * (c + 1)],
+                        start=(g == 0),
+                        stop=(g == JG - 1),
+                    )
+                nc.vector.tensor_scalar(
+                    out=n_t[:, 512 * c : 512 * (c + 1)], in0=acc[:], scalar1=-SCALE, scalar2=None,
+                    op0=ALU.mult, op1=ALU.min, accum_out=vs[:, c : c + 1],
+                )
+            negm = gs[:, 0:1]
+            nc.gpsimd.tensor_scalar(out=negm, in0=vs[:, 0:1], scalar1=vs[:, 1:2], scalar2=vs[:, 2:3], op0=ALU.min, op1=ALU.min)
+
+        def exps(i):
+            vs, gs = stats[i]
+            n_t = neg[i]
+            negm = gs[:, 0:1]
+            junk = stage.tile([P, V], BF16, name="junk", tag="junk", bufs=1)
+            ssum = vs[:, 3:4]
+            nc.scalar.activation(out=junk[:], in_=n_t[:], func=ACT.Exp, bias=negm, scale=-1.0, accum_out=ssum)
+
+        def logs(i):
+            vs, gs = stats[i]
+            negm, ssum = gs[:, 0:1], vs[:, 3:4]
+            up, down, ngs = gs[:, 9:10], gs[:, 10:11], gs[:, 11:12]
+            nc.gpsimd.tensor_tensor(out=up, in0=ssum, in1=expo[:, 0:1], op=ALU.pow)
+            nc.gpsimd.tensor_tensor(out=down, in0=ssum, in1=expo[:, 1:2], op=ALU.pow)
+            nc.gpsimd.tensor_scalar(out=down, in0=down, scalar1=32.0, scalar2=0.0, op0=ALU.mult, op1=ALU.add)
+            nc.gpsimd.tensor_scalar(out=ngs, in0=up, scalar1=-32.0, scalar2=down, op0=ALU.mult, op1=ALU.add)
+            ey = vs[:, 5:6]
+            nc.scalar.activation(out=ey, in_=ngs, func=ACT.Exp, scale=1.0)
+            base, base2, d = gs[:, 1:2], gs[:, 2:3], gs[:, 3:4]
+            ts = nc.gpsimd.tensor_scalar
+            ts(out=base, in0=negm, scalar1=1.0, scalar2=math.log(V), op0=ALU.mult, op1=ALU.add)
+            ts(out=base2, in0=ngs, scalar1=1.0, scalar2=base, op0=ALU.mult, op1=ALU.add)
+            ts(out=d, in0=ey, scalar1=ssum, scalar2=-1.0, op0=ALU.mult, op1=ALU.add)
+            p = [gs[:, 4 + k : 5 + k] for k in range(4)]
+            ts(out=p[0], in0=d, scalar1=-0.2, scalar2=0.25, op0=ALU.mult, op1=ALU.add)
+            ts(out=p[1], in0=p[0], scalar1=d, scalar2=-1.0 / 3.0, op0=ALU.mult, op1=ALU.add)
+            ts(out=p[2], in0=p[1], scalar1=d, scalar2=0.5, op0=ALU.mult, op1=ALU.add)
+            ts(out=p[3], in0=p[2], scalar1=d, scalar2=-1.0, op0=ALU.mult, op1=ALU.add)
+            c_t = gs[:, 8:9]
+            ts(out=c_t, in0=p[3], scalar1=d, scalar2=base2, op0=ALU.mult, op1=ALU.add)
+            cvals[i] = c_t
+
+        def final_b(i):
+            ob = stage.tile([P, V], BF16, name="ob", tag="ob", align_bytes=64)
+            outb[i] = ob
+            nc.vector.tensor_scalar(out=ob[:], in0=neg[i][:], scalar1=-1.0, scalar2=cvals[i], op0=ALU.mult, op1=ALU.add)
+
+        def final_f(i):
+            of = stage.tile([P, V], F32, name="of", tag="of")
+            if FINAL_ON[i] == "V":
+                nc.vector.tensor_scalar(out=of[:], in0=neg[i][:], scalar1=-1.0, scalar2=cvals[i], op0=ALU.mult, op1=ALU.add)
+            elif FINAL_ON[i] == "G":
+                nc.gpsimd.tensor_scalar(out=of[:], in0=neg[i][:], scalar1=-1.0, scalar2=cvals[i], op0=ALU.mult, op1=ALU.add)
+            else:
+                nc.scalar.activation(out=of[:], in_=neg[i][:], func=ACT.Identity, bias=cvals[i], scale=-1.0)
+            nc.sync.dma_start(out=out[P * i : P * (i + 1), :], in_=of[:])
+
+        p_grouped = {}
+
+        def turn(i):
+            words = outb[i][:].bitcast(F32)
+            grouped = stage.tile([P, VG, P, 4], BF16, name="p_grouped", tag="p_grouped", align_bytes=64)
+            p_grouped[i] = grouped
+            for g0, g1 in ((0, 2), (2, 3)):
+                tp = psum_t.tile([P, 2, 2, P], F32, name="tpp", tag="tp")
+                for g in range(g0, g1):
+                    for u in range(2):
+                        nc.tensor.transpose(tp[:, g - g0, u, :], words[:, 256 * g + u : 256 * (g + 1) : 2], ident[:])
+                nc.scalar.copy(
+                    out=grouped[:, g0:g1].rearrange("p g r t -> p g (r t)").bitcast(F32).rearrange("p g (r u) -> p g r u", u=2),
+                    in_=tp[:, 0 : g1 - g0].rearrange("p g u r -> p g r u"),
+                )
+
+        def plane_quant(i):
+            codes = stage.tile([P, VG, P], I32, name="p_codes", tag="p_codes", align_bytes=64)
+            for g in range(VG):
+                nc.vector.quantize_mx(
+                    out=codes[:, g, :].bitcast(FP8X4),
+                    scales=plane_scales[:, g, P * i : P * (i + 1)],
+                    in_=p_grouped[i][:, g].rearrange("p r t -> p (r t)"),
+                )
+            nc.sync.dma_start(
+                out=out_words.rearrange("g p m t -> p g (m t)")[:, :, 512 * i : 512 * (i + 1)].bitcast(I32),
+                in_=codes[:],
+            )
+
+        def store_scales(m0, m1):
+            for q in range(4):
+                nc.sync.dma_start(
+                    out=out_scales.rearrange("g q m -> q g m")[4 * q : 4 * q + 4, :, m0:m1].bitcast(I32),
+                    in_=plane_scales[32 * q : 32 * q + 4, :, m0:m1].bitcast(I32),
+                )
+
+        FINAL_ON = "SSSSSVSV"
+        units = [
+            label_unit(0, 256, 0), label_unit(256, 256, 0), label_unit(512, 512, 0), label_unit(0, 512, 1), label_unit(512, 512, 1),
+            context_unit(0, 512, 0), context_unit(0, 512, 1), label_unit(1024, 512, 0), label_unit(1024, 512, 1),
+            context_unit(512, 512, 0), context_unit(512, 512, 1),
+        ]
+        permute_scales(0)
+        permute_words(u_codes, u_raw, 0)
+        project(units[0])
+        permute_scales(1)
+        project(units[1])
+        gain(units[0])
+        permute_words(u_codes, u_raw, 1)
+        project(units[2])
+        gain(units[1])
+        quant(units[0])
+        quant(units[1])
+        permute_words(vp_codes, vp_raw, 0)
+        project(units[3])
+        h_turn(0)
+        h_turn(1)
+        gain(units[2], 0, 2)
+        permute_words(vp_codes, vp_raw, 1)
+        gain(units[2], 1, 2)
+        project(units[4])
+        h_turn(2)
+        h_turn(3)
+        gain(units[3], 0, 2)
+        quant(units[2])
+        gain(units[3], 1, 2)
+        h_quant(0, 0)
+        h_quant(0, 1)
+        project(units[5])
+        gain(units[4], 0, 2)
+        quant(units[3])
+        gain(units[4], 1, 2)
+        project(units[6])
+        h_turn(4)
+        h_turn(5)
+        gain(units[5], 0, 2)
+        quant(units[4])
+        gain(units[5], 1, 2)
+        project(units[7])
+        h_turn(6)
+        h_turn(7)
+        gain(units[6], 0, 2)
+        quant(units[5])
+        gain(units[6], 1, 2)
+        project(units[8])
+        gain(units[7], 0, 2)
+        quant(units[6])
+        h_quant(1, 0)
+        h_quant(1, 1)
+        gain(units[7], 1, 2)
+        project(units[9])
+        gain(units[8], 0, 2)
+        quant(units[7])
+        gain(units[8], 1, 2)
+        project(units[10])
+        gain(units[9], 0, 2)
+        quant(units[8])
+        scores(0)
+        exps(0)
+        scores(1)
+        exps(1)
+        gain(units[9], 1, 2)
+        logs(0)
+        scores(2)
+        exps(2)
+        logs(1)
+        quant(units[9])
+        final_b(0)
+        final_f(0)
+        gain(units[10], 0, 2)
+        scores(3)
+        turn(0)
+        final_f(1)
+        logs(2)
+        exps(3)
+        final_b(1)
+        gain(units[10], 1, 2)
+        plane_quant(0)
+        logs(3)
+        quant(units[10])
+        turn(1)
+        final_b(2)
+        final_f(2)
+        for i in range(4, NT):
+            scores(i)
+            turn(i - 2)
+            exps(i)
+            plane_quant(i - 3)
+            final_b(i - 1)
+            final_f(i - 1)
+            logs(i)
+            if i == 6:
+                store_scales(0, 512)
+        final_b(NT - 1)
+        turn(NT - 2)
+        final_f(NT - 1)
+        plane_quant(NT - 3)
+        turn(NT - 1)
+        plane_quant(NT - 2)
+        plane_quant(NT - 1)
+        store_scales(512, 1024)

@@ -15,12 +15,15 @@ AX = mybir.AxisListType
 
 P = 128
 N, D, J, V = 1024, 1024, 1024, 1536
-KG = 2
-JG = 2
-VG = V // 512
-NT = N // P
-SCALE = 2.0 / math.sqrt(J)
-LN2 = math.log(2.0)
+SLOTS = 4
+GROUP = P * SLOTS
+D_GROUPS, J_GROUPS, V_GROUPS = D // GROUP, J // GROUP, V // GROUP
+RUN = 8
+TOKEN_TILES = N // P
+BATCH = 4
+SCORE_SCALE = 2.0 / math.sqrt(J)
+LABEL_BIAS, CONTEXT_BIAS, LABEL_GAIN, CONTEXT_GAIN = 0, 2, 4, 6
+
 FLOPS = 2 * (V * D * J + N * D * J + N * J * V)
 
 
@@ -28,395 +31,403 @@ def tile_jointinputoutputembeddingtiedhead_x2_kernel(
     tc, h, emb_words, emb_scales, u_words, u_scales, vp_words, vp_scales, bj, gu, gv, out, out_words, out_scales
 ):
     nc = tc.nc
-    ctx_stack = ExitStack()
-    with ctx_stack as es:
-        keep = es.enter_context(tc.tile_pool(name="keep", bufs=1))
-        stage = es.enter_context(tc.tile_pool(name="stage", bufs=3))
-        small = es.enter_context(tc.tile_pool(name="small", bufs=8))
-        psum = es.enter_context(tc.psum_pool(name="psum", bufs=6))
-        psum_t = es.enter_context(tc.psum_pool(name="psum_t", bufs=2))
-        es.enter_context(tc.manual_schedule())
+    with ExitStack() as stack:
+        keep = stack.enter_context(tc.tile_pool(name="keep", bufs=1))
+        stage = stack.enter_context(tc.tile_pool(name="stage", bufs=3))
+        sums_psum = stack.enter_context(tc.psum_pool(name="sums_psum", bufs=6))
+        turn_psum = stack.enter_context(tc.psum_pool(name="turn_psum", bufs=2))
+        stack.enter_context(tc.manual_schedule())
 
-        rows = keep.tile([P, 512], BF16, name="rows")
-        nc.gpsimd.memset(rows[:], 0.0)
-        uv_packed = keep.tile([P, J], U8, name="uv_packed", align_bytes=64)
-        nc.vector.memset(uv_packed[:].bitcast(I32), 0)
-        emb_packed = keep.tile([P, V], U8, name="emb_packed", align_bytes=64)
-        nc.vector.memset(emb_packed[:].bitcast(I32), 0)
+        vector_rows = keep.tile([P, GROUP], BF16, name="vector_rows")
+        nc.gpsimd.memset(vector_rows[:], 0.0)
 
-        nc.scalar.dma_start(out=rows[0:4, :], in_=bj.rearrange("v (g x) -> (v g) x", g=JG))
-        nc.scalar.dma_start(out=rows[4:6, :], in_=gu.rearrange("(g x) -> g x", g=JG))
-        nc.scalar.dma_start(out=rows[6:8, :], in_=gv.rearrange("(g x) -> g x", g=JG))
+        arrived_scales = {}
+        for name, width in (("u", J), ("emb", V), ("vp", J)):
+            arrived_scales[name] = keep.tile([P, width], U8, name=f"{name}_arrived_scales", align_bytes=64)
+            nc.vector.memset(arrived_scales[name][:].bitcast(I32), 0)
 
-        for q in range(4):
-            nc.sync.dma_start(out=uv_packed[32 * q : 32 * q + 8, :].bitcast(I32), in_=u_scales[:, 4 * q : 4 * q + 4, :].bitcast(I32))
-            nc.sync.dma_start(out=uv_packed[32 * q + 8 : 32 * q + 16, :].bitcast(I32), in_=vp_scales[:, 4 * q : 4 * q + 4, :].bitcast(I32))
-            nc.sync.dma_start(out=emb_packed[32 * q : 32 * q + 8, :].bitcast(I32), in_=emb_scales[:, 4 * q : 4 * q + 4, :].bitcast(I32))
+        arrived_words = {}
+        for name in ("u", "vp"):
+            arrived_words[name] = stage.tile([P, D_GROUPS, J], I32, name=f"{name}_arrived", tag="tanh", bufs=5, align_bytes=64)
+        emb_codes = keep.tile([P, D_GROUPS, V], I32, name="emb_codes", align_bytes=64)
+        h_rows = [keep.tile([P, D], BF16, name=f"h_rows{i}", align_bytes=64) for i in range(TOKEN_TILES)]
 
-        u_raw = keep.tile([P, KG, J], I32, name="u_raw", align_bytes=64)
-        vp_raw = keep.tile([P, KG, J], I32, name="vp_raw", align_bytes=64)
-        emb_codes = keep.tile([P, KG, V], I32, name="emb_codes", align_bytes=64)
-        h_raw = [keep.tile([P, D], BF16, name=f"h_raw{i}", align_bytes=64) for i in range(NT)]
+        nc.scalar.dma_start(out=vector_rows[0:4, :], in_=bj.rearrange("v (g x) -> (v g) x", g=J_GROUPS))
+        nc.scalar.dma_start(out=vector_rows[4:6, :], in_=gu.rearrange("(g x) -> g x", g=J_GROUPS))
+        nc.scalar.dma_start(out=vector_rows[6:8, :], in_=gv.rearrange("(g x) -> g x", g=J_GROUPS))
 
-        def load_words(tile, words, g, c0, c1):
-            nc.sync.dma_start(out=tile[:, g, c0:c1], in_=words[g].rearrange("p n t -> p (n t)")[:, 4 * c0 : 4 * c1].bitcast(I32))
+        def load_scales(name, scales):
+            for q in range(4):
+                nc.sync.dma_start(
+                    out=arrived_scales[name][32 * q : 32 * q + 8, :].bitcast(I32),
+                    in_=scales[:, 4 * q : 4 * q + 4, :].bitcast(I32),
+                )
+
+        def load_words(tile, words, c0, c1):
+            for g in range(D_GROUPS):
+                nc.sync.dma_start(
+                    out=tile[:, g, c0:c1],
+                    in_=words[g].rearrange("p n t -> p (n t)")[:, SLOTS * c0 : SLOTS * c1].bitcast(I32),
+                )
 
         def load_h(i):
-            nc.sync.dma_start(out=h_raw[i][:], in_=h[P * i : P * (i + 1), :])
+            nc.sync.dma_start(out=h_rows[i][:], in_=h[P * i : P * (i + 1), :])
 
-        for g in range(KG):
-            load_words(u_raw, u_words, g, 0, 512)
-        for c0, c1 in ((0, 256), (256, 512), (512, 1024)):
-            for g in range(KG):
-                load_words(emb_codes, emb_words, g, c0, c1)
-        for g in range(KG):
-            load_words(u_raw, u_words, g, 512, 1024)
-        for g in range(KG):
-            load_words(vp_raw, vp_words, g, 0, 1024)
+        load_scales("u", u_scales)
+        load_scales("emb", emb_scales)
+        load_words(arrived_words["u"], u_words, 0, 512)
+        load_words(emb_codes, emb_words, 0, 256)
+        load_words(emb_codes, emb_words, 256, 512)
+        load_words(emb_codes, emb_words, 512, 1024)
+        load_words(arrived_words["u"], u_words, 512, 1024)
+        load_scales("vp", vp_scales)
+        load_words(arrived_words["vp"], vp_words, 0, 1024)
         for i in range(4):
             load_h(i)
-        for g in range(KG):
-            load_words(emb_codes, emb_words, g, 1024, 1536)
-        for i in range(4, 8):
+        load_words(emb_codes, emb_words, 1024, 1536)
+        for i in range(4, TOKEN_TILES):
             load_h(i)
 
-        expo = keep.tile([P, 2], F32, name="expo")
-        nc.gpsimd.memset(expo[:, 0:1], 1.0 / 64.0)
-        nc.gpsimd.memset(expo[:, 1:2], -1.0 / 64.0)
-        ident = keep.tile([P, P], F32, name="ident")
-        make_identity(nc, ident[:])
+        identity = keep.tile([P, P], F32, name="identity")
+        make_identity(nc, identity[:])
 
-        rows_p = keep.tile([P, 512], F32, name="rows_p")
-        nc.vector.tensor_copy(
-            out=rows_p[:].rearrange("p (t b i) -> p t b i", t=4, i=8),
-            in_=rows[:].rearrange("p (b t i) -> p t b i", t=4, i=8),
-        )
-        cols_ps = psum_t.tile([P, 4, P], F32, name="cols_ps", tag="tp")
-        for t in range(4):
-            nc.tensor.transpose(cols_ps[:, t, :], rows_p[:, P * t : P * (t + 1)], ident[:])
-        cols = keep.tile([P, 8, 4], F32, name="cols")
-        nc.scalar.copy(out=cols[:], in_=cols_ps[:, :, 0:8].rearrange("p t r -> p r t"))
+        slotted_rows = keep.tile([P, GROUP], F32, name="slotted_rows")
+        columns = keep.tile([P, 8, SLOTS], F32, name="columns")
 
-        uv_scales = keep.tile([P, JG, 4, P], U8, name="uv_scales", align_bytes=64)
-        u_codes = keep.tile([P, KG, JG, 4, P], I32, name="u_codes", align_bytes=64)
-        vp_codes = keep.tile([P, KG, JG, 4, P], I32, name="vp_codes", align_bytes=64)
-
-        def permute(dst, source):
+        def spread_vectors():
             nc.vector.tensor_copy(
-                out=dst.rearrange("p t (b i) -> p t b i", i=8),
-                in_=source.rearrange("p (b t i) -> p t b i", t=4, i=8),
+                out=slotted_rows[:].rearrange("p (t b i) -> p t b i", t=SLOTS, i=RUN),
+                in_=vector_rows[:].rearrange("p (b t i) -> p t b i", t=SLOTS, i=RUN),
+            )
+            turned = turn_psum.tile([P, SLOTS, P], F32, name="turned_rows", tag="turn")
+            for t in range(SLOTS):
+                nc.tensor.transpose(turned[:, t, :], slotted_rows[:, P * t : P * (t + 1)], identity[:])
+            nc.scalar.copy(out=columns[:], in_=turned[:, :, 0:8].rearrange("p t r -> p r t"))
+
+        weight_codes = {
+            name: keep.tile([P, D_GROUPS, SLOTS, J // SLOTS], I32, name=f"{name}_codes", align_bytes=64) for name in ("u", "vp")
+        }
+        weight_scales = {name: keep.tile([P, SLOTS, J // SLOTS], U8, name=f"{name}_scales", align_bytes=64) for name in ("u", "vp")}
+
+        def slot_words(name, g, c0, c1):
+            nc.vector.tensor_copy(
+                out=weight_codes[name][:, g, :, c0 // SLOTS : c1 // SLOTS].rearrange("p t (b i) -> p t b i", i=RUN),
+                in_=arrived_words[name][:, g, c0:c1].rearrange("p (b t i) -> p t b i", t=SLOTS, i=RUN),
             )
 
-        def permute_words(dst, raw, gj):
-            for g in range(KG):
-                permute(dst[:, g, gj], raw[:, g, 512 * gj : 512 * (gj + 1)])
-
-        def permute_scales(gj):
-            permute(uv_scales[:, gj], uv_packed[:, 512 * gj : 512 * (gj + 1)])
-
-        lab_codes = keep.tile([P, JG, V], I32, name="lab_codes", align_bytes=64)
-        lab_scales = keep.tile([P, JG, V], U8, name="lab_scales", align_bytes=64)
-        h_codes = keep.tile([P, KG, N], I32, name="h_codes", align_bytes=64)
-        h_scales = keep.tile([P, KG, N], U8, name="h_scales", align_bytes=64)
-        ctx_codes = keep.tile([P, JG, N], I32, name="ctx_codes", align_bytes=64)
-        ctx_scales = keep.tile([P, JG, N], U8, name="ctx_scales", align_bytes=64)
-        plane_scales = keep.tile([P, VG, N], U8, name="plane_scales", align_bytes=64)
-
-        th_t = {}
-        gained_t = {}
-
-        def label_unit(c0, w, gj):
-            return ("lab", c0, w, gj)
-
-        def context_unit(c0, w, gj):
-            return ("ctx", c0, w, gj)
-
-        def project(unit):
-            kind, c0, w, gj = unit
-            codes_w, plane0, bias_row = (u_codes, 0, 0) if kind == "lab" else (vp_codes, 8, 2)
-            th = stage.tile([P, 4, w], F32, name="th", tag="th", bufs=3)
-            th_t[unit] = th
-            for t in range(4):
-                acc = psum.tile([P, w], F32, name="acc", tag="acc")
-                for g in range(KG):
-                    if kind == "lab":
-                        rhs, rhs_scale = emb_codes[:, g, c0 : c0 + w], emb_packed[4 * g :, c0 : c0 + w]
-                    else:
-                        rhs, rhs_scale = h_codes[:, g, c0 : c0 + w], h_scales[:, g, c0 : c0 + w]
-                    nc.tensor.matmul_mx(
-                        out=acc[:],
-                        lhsT=codes_w[:, g, gj, t, :].bitcast(FP8X4),
-                        lhsT_scale=uv_scales[plane0 + 4 * g :, gj, t, :],
-                        rhs=rhs.bitcast(FP8X4),
-                        rhs_scale=rhs_scale,
-                        start=(g == 0),
-                        stop=(g == KG - 1),
-                    )
-                nc.scalar.activation(out=th[:, t, :], in_=acc[:], func=ACT.Tanh, bias=cols[:, bias_row + gj, t : t + 1], scale=1.0)
-
-        def gain(unit, part=0, parts=1):
-            kind, c0, w, gj = unit
-            if part == 0:
-                gained_t[unit] = stage.tile([P, w, 4], BF16, name="gained", tag="gained", align_bytes=64)
-            gain_row = 4 if kind == "lab" else 6
-            n = w // parts
-            cs = slice(n * part, n * (part + 1))
-            nc.vector.tensor_tensor(
-                out=gained_t[unit][:, cs, :].rearrange("p (c i) t -> p c t i", i=4),
-                in0=th_t[unit][:, :, cs].rearrange("p t (c i) -> p c t i", i=4),
-                in1=cols[:, gain_row + gj, :].unsqueeze(1).unsqueeze(3).to_broadcast([P, n // 4, 4, 4]),
-                op=ALU.mult,
+        def slot_scales(name):
+            nc.vector.tensor_copy(
+                out=weight_scales[name][:].rearrange("p t m -> p (t m)").bitcast(I32).rearrange("p (t b i) -> p t b i", t=SLOTS, i=2),
+                in_=arrived_scales[name][:].bitcast(I32).rearrange("p (b t i) -> p t b i", t=SLOTS, i=2),
             )
 
-        def quant(unit):
-            kind, c0, w, gj = unit
-            codes, scales = (lab_codes, lab_scales) if kind == "lab" else (ctx_codes, ctx_scales)
-            nc.vector.quantize_mx(
-                out=codes[:, gj, c0 : c0 + w].bitcast(FP8X4),
-                scales=scales[:, gj, c0 : c0 + w],
-                in_=gained_t[unit][:].rearrange("p c t -> p (c t)"),
-            )
+        h_codes = keep.tile([P, D_GROUPS, N], I32, name="h_codes", align_bytes=64)
+        h_scales = keep.tile([P, D_GROUPS, N], U8, name="h_scales", align_bytes=64)
+        label_codes = keep.tile([P, J_GROUPS, V], I32, name="label_codes", align_bytes=64)
+        label_scales = keep.tile([P, J_GROUPS, V], U8, name="label_scales", align_bytes=64)
+        context_codes = keep.tile([P, J_GROUPS, N], I32, name="context_codes", align_bytes=64)
+        context_scales = keep.tile([P, J_GROUPS, N], U8, name="context_scales", align_bytes=64)
+        result_scales = keep.tile([P, V_GROUPS, N], U8, name="result_scales", align_bytes=64)
 
         h_grouped = {}
 
-        def h_turn(k):
-            if k % 4 == 0:
-                h_grouped[k // 4] = stage.tile([P, KG, 512, 4], BF16, name="h_grouped", tag="h_grouped", bufs=2, align_bytes=64)
-            grouped = h_grouped[k // 4]
-            words = h_raw[k][:].bitcast(F32)
-            xt = psum_t.tile([P, KG, 2, P], F32, name="xt", tag="tp")
-            for g in range(KG):
-                for u in range(2):
-                    nc.tensor.transpose(xt[:, g, u, :], words[:, 256 * g + u : 256 * (g + 1) : 2], ident[:])
-            r0 = P * (k % 4)
+        def turn_words(words, turned, group):
+            for u in range(2):
+                nc.tensor.transpose(turned[:, u, :], words[:, 256 * group + u : 256 * (group + 1) : 2], identity[:])
+
+        def turn_h(i):
+            half, row0 = i // 4, P * (i % 4)
+            if i % 4 == 0:
+                h_grouped[half] = stage.tile([P, D_GROUPS, 512, SLOTS], BF16, name="h_grouped", tag="h_grouped", bufs=1, align_bytes=64)
+            turned = turn_psum.tile([P, D_GROUPS, 2, P], F32, name="turned_h", tag="turn")
+            for g in range(D_GROUPS):
+                turn_words(h_rows[i][:].bitcast(F32), turned[:, g], g)
             nc.scalar.copy(
-                out=grouped[:, :, r0 : r0 + P, :].rearrange("p g r t -> p g (r t)").bitcast(F32).rearrange("p g (r u) -> p g r u", u=2),
-                in_=xt[:].rearrange("p g u r -> p g r u"),
+                out=h_grouped[half][:, :, row0 : row0 + P, :]
+                .rearrange("p g r t -> p g (r t)")
+                .bitcast(F32)
+                .rearrange("p g (r u) -> p g r u", u=2),
+                in_=turned[:].rearrange("p g u r -> p g r u"),
             )
 
-        def h_quant(hh, g):
-            nc.vector.quantize_mx(
-                out=h_codes[:, g, 512 * hh : 512 * (hh + 1)].bitcast(FP8X4),
-                scales=h_scales[:, g, 512 * hh : 512 * (hh + 1)],
-                in_=h_grouped[hh][:, g].rearrange("p r t -> p (r t)"),
-            )
+        def quantise_h(half):
+            cols = slice(512 * half, 512 * (half + 1))
+            for g in range(D_GROUPS):
+                nc.vector.quantize_mx(
+                    out=h_codes[:, g, cols].bitcast(FP8X4),
+                    scales=h_scales[:, g, cols],
+                    in_=h_grouped[half][:, g].rearrange("p r t -> p (r t)"),
+                )
 
-        neg = {}
-        cvals = {}
-        outb = {}
+        label_blocks = [
+            ("label", 0, 256, 0),
+            ("label", 256, 256, 0),
+            ("label", 512, 512, 0),
+            ("label", 0, 512, 1),
+            ("label", 512, 512, 1),
+            ("label", 1024, 512, 0),
+            ("label", 1024, 512, 1),
+        ]
+        context_blocks = [("context", 512 * half, 512, group) for half in range(2) for group in range(J_GROUPS)]
+        gain_on_scalar = context_blocks[2]
 
-        stats = {}
+        tanh_tiles, scaled_tiles, grouped_tiles = {}, {}, {}
 
-        def scores(i):
-            n_t = stage.tile([P, V], F32, name="neg", tag="neg", bufs=4)
-            neg[i] = n_t
-            vs = small.tile([P, 8], F32, name="vs", tag="vs")
-            gs = small.tile([P, 16], F32, name="gs", tag="gs")
-            stats[i] = (vs, gs)
-            for c in range(VG):
-                acc = psum.tile([P, 512], F32, name="accs", tag="acc")
-                for g in range(JG):
+        def project(block):
+            side, c0, width, group = block
+            cols = slice(c0, c0 + width)
+            if side == "label":
+                weight, bias, gain, codes, scales = "u", LABEL_BIAS, LABEL_GAIN, emb_codes, None
+            else:
+                weight, bias, gain, codes, scales = "vp", CONTEXT_BIAS, CONTEXT_GAIN, h_codes, h_scales
+            tanh_tiles[block] = stage.tile([P, SLOTS, width], F32, name="tanh", tag="tanh", bufs=5, align_bytes=64)
+            if block == gain_on_scalar:
+                scaled_tiles[block] = stage.tile([P, SLOTS, width], BF16, name="scaled", tag="rounded", bufs=3, align_bytes=64)
+            for t in range(SLOTS):
+                acc = sums_psum.tile([P, width], F32, name="acc", tag="acc")
+                for g in range(D_GROUPS):
                     nc.tensor.matmul_mx(
                         out=acc[:],
-                        lhsT=ctx_codes[:, g, P * i : P * (i + 1)].bitcast(FP8X4),
-                        lhsT_scale=ctx_scales[:, g, P * i : P * (i + 1)],
-                        rhs=lab_codes[:, g, 512 * c : 512 * (c + 1)].bitcast(FP8X4),
-                        rhs_scale=lab_scales[:, g, 512 * c : 512 * (c + 1)],
+                        lhsT=weight_codes[weight][:, g, t, P * group : P * (group + 1)].bitcast(FP8X4),
+                        lhsT_scale=weight_scales[weight][4 * g :, t, P * group : P * (group + 1)],
+                        rhs=codes[:, g, cols].bitcast(FP8X4),
+                        rhs_scale=arrived_scales["emb"][4 * g :, cols] if scales is None else scales[:, g, cols],
                         start=(g == 0),
-                        stop=(g == JG - 1),
+                        stop=(g == D_GROUPS - 1),
                     )
-                nc.vector.tensor_scalar(
-                    out=n_t[:, 512 * c : 512 * (c + 1)], in0=acc[:], scalar1=-SCALE, scalar2=None,
-                    op0=ALU.mult, op1=ALU.min, accum_out=vs[:, c : c + 1],
+                nc.scalar.activation(
+                    out=tanh_tiles[block][:, t, :], in_=acc[:], func=ACT.Tanh, bias=columns[:, bias + group, t : t + 1], scale=1.0
                 )
-            negm = gs[:, 0:1]
-            nc.gpsimd.tensor_scalar(out=negm, in0=vs[:, 0:1], scalar1=vs[:, 1:2], scalar2=vs[:, 2:3], op0=ALU.min, op1=ALU.min)
+                if block == gain_on_scalar:
+                    nc.scalar.activation(
+                        out=scaled_tiles[block][:, t, :],
+                        in_=tanh_tiles[block][:, t, :],
+                        func=ACT.Copy,
+                        scale=columns[:, gain + group, t : t + 1],
+                    )
 
-        def exps(i):
-            vs, gs = stats[i]
-            n_t = neg[i]
-            negm = gs[:, 0:1]
-            junk = stage.tile([P, V], BF16, name="junk", tag="junk", bufs=1)
-            ssum = vs[:, 3:4]
-            nc.scalar.activation(out=junk[:], in_=n_t[:], func=ACT.Exp, bias=negm, scale=-1.0, accum_out=ssum)
-
-        def logs(i):
-            vs, gs = stats[i]
-            negm, ssum = gs[:, 0:1], vs[:, 3:4]
-            up, down, ngs = gs[:, 9:10], gs[:, 10:11], gs[:, 11:12]
-            nc.gpsimd.tensor_tensor(out=up, in0=ssum, in1=expo[:, 0:1], op=ALU.pow)
-            nc.gpsimd.tensor_tensor(out=down, in0=ssum, in1=expo[:, 1:2], op=ALU.pow)
-            nc.gpsimd.tensor_scalar(out=down, in0=down, scalar1=32.0, scalar2=0.0, op0=ALU.mult, op1=ALU.add)
-            nc.gpsimd.tensor_scalar(out=ngs, in0=up, scalar1=-32.0, scalar2=down, op0=ALU.mult, op1=ALU.add)
-            ey = vs[:, 5:6]
-            nc.scalar.activation(out=ey, in_=ngs, func=ACT.Exp, scale=1.0)
-            base, base2, d = gs[:, 1:2], gs[:, 2:3], gs[:, 3:4]
-            ts = nc.gpsimd.tensor_scalar
-            ts(out=base, in0=negm, scalar1=1.0, scalar2=math.log(V), op0=ALU.mult, op1=ALU.add)
-            ts(out=base2, in0=ngs, scalar1=1.0, scalar2=base, op0=ALU.mult, op1=ALU.add)
-            ts(out=d, in0=ey, scalar1=ssum, scalar2=-1.0, op0=ALU.mult, op1=ALU.add)
-            p = [gs[:, 4 + k : 5 + k] for k in range(4)]
-            ts(out=p[0], in0=d, scalar1=-0.2, scalar2=0.25, op0=ALU.mult, op1=ALU.add)
-            ts(out=p[1], in0=p[0], scalar1=d, scalar2=-1.0 / 3.0, op0=ALU.mult, op1=ALU.add)
-            ts(out=p[2], in0=p[1], scalar1=d, scalar2=0.5, op0=ALU.mult, op1=ALU.add)
-            ts(out=p[3], in0=p[2], scalar1=d, scalar2=-1.0, op0=ALU.mult, op1=ALU.add)
-            c_t = gs[:, 8:9]
-            ts(out=c_t, in0=p[3], scalar1=d, scalar2=base2, op0=ALU.mult, op1=ALU.add)
-            cvals[i] = c_t
-
-        def final_b(i):
-            ob = stage.tile([P, V], BF16, name="ob", tag="ob", align_bytes=64)
-            outb[i] = ob
-            nc.vector.tensor_scalar(out=ob[:], in0=neg[i][:], scalar1=-1.0, scalar2=cvals[i], op0=ALU.mult, op1=ALU.add)
-
-        def final_f(i):
-            of = stage.tile([P, V], F32, name="of", tag="of")
-            if FINAL_ON[i] == "V":
-                nc.vector.tensor_scalar(out=of[:], in0=neg[i][:], scalar1=-1.0, scalar2=cvals[i], op0=ALU.mult, op1=ALU.add)
-            elif FINAL_ON[i] == "G":
-                nc.gpsimd.tensor_scalar(out=of[:], in0=neg[i][:], scalar1=-1.0, scalar2=cvals[i], op0=ALU.mult, op1=ALU.add)
-            else:
-                nc.scalar.activation(out=of[:], in_=neg[i][:], func=ACT.Identity, bias=cvals[i], scale=-1.0)
-            nc.sync.dma_start(out=out[P * i : P * (i + 1), :], in_=of[:])
-
-        p_grouped = {}
-
-        def turn(i):
-            words = outb[i][:].bitcast(F32)
-            grouped = stage.tile([P, VG, P, 4], BF16, name="p_grouped", tag="p_grouped", align_bytes=64)
-            p_grouped[i] = grouped
-            for g0, g1 in ((0, 2), (2, 3)):
-                tp = psum_t.tile([P, 2, 2, P], F32, name="tpp", tag="tp")
-                for g in range(g0, g1):
-                    for u in range(2):
-                        nc.tensor.transpose(tp[:, g - g0, u, :], words[:, 256 * g + u : 256 * (g + 1) : 2], ident[:])
-                nc.scalar.copy(
-                    out=grouped[:, g0:g1].rearrange("p g r t -> p g (r t)").bitcast(F32).rearrange("p g (r u) -> p g r u", u=2),
-                    in_=tp[:, 0 : g1 - g0].rearrange("p g u r -> p g r u"),
+        def apply_gain(block):
+            side, c0, width, group = block
+            gain = LABEL_GAIN if side == "label" else CONTEXT_GAIN
+            grouped = stage.tile([P, width, SLOTS], BF16, name="grouped", tag="grouped", align_bytes=64)
+            grouped_tiles[block] = grouped
+            if block == gain_on_scalar:
+                nc.vector.tensor_copy(
+                    out=grouped[:].rearrange("p (c i) t -> p c t i", i=4),
+                    in_=scaled_tiles[block][:].rearrange("p t (c i) -> p c t i", i=4),
                 )
-
-        def plane_quant(i):
-            codes = stage.tile([P, VG, P], I32, name="p_codes", tag="p_codes", align_bytes=64)
-            for g in range(VG):
-                nc.vector.quantize_mx(
-                    out=codes[:, g, :].bitcast(FP8X4),
-                    scales=plane_scales[:, g, P * i : P * (i + 1)],
-                    in_=p_grouped[i][:, g].rearrange("p r t -> p (r t)"),
-                )
-            nc.sync.dma_start(
-                out=out_words.rearrange("g p m t -> p g (m t)")[:, :, 512 * i : 512 * (i + 1)].bitcast(I32),
-                in_=codes[:],
+                return
+            nc.vector.tensor_tensor(
+                out=grouped[:].rearrange("p (c i) t -> p c t i", i=2),
+                in0=tanh_tiles[block][:].rearrange("p t (c i) -> p c t i", i=2),
+                in1=columns[:, gain + group, :].unsqueeze(1).unsqueeze(3).to_broadcast([P, width // 2, SLOTS, 2]),
+                op=ALU.mult,
             )
 
-        def store_scales(m0, m1):
-            for q in range(4):
-                nc.sync.dma_start(
-                    out=out_scales.rearrange("g q m -> q g m")[4 * q : 4 * q + 4, :, m0:m1].bitcast(I32),
-                    in_=plane_scales[32 * q : 32 * q + 4, :, m0:m1].bitcast(I32),
+        def quantise(block):
+            side, c0, width, group = block
+            codes, scales = (label_codes, label_scales) if side == "label" else (context_codes, context_scales)
+            nc.vector.quantize_mx(
+                out=codes[:, group, c0 : c0 + width].bitcast(FP8X4),
+                scales=scales[:, group, c0 : c0 + width],
+                in_=grouped_tiles[block][:].rearrange("p c t -> p (c t)"),
+            )
+
+        negated, rounded, result_grouped, result_codes = {}, {}, {}, {}
+        batches = range(TOKEN_TILES // BATCH)
+        minima = [keep.tile([P, BATCH, V_GROUPS], F32, name=f"minima{b}") for b in batches]
+        minus_max = [keep.tile([P, BATCH], F32, name=f"minus_max{b}") for b in batches]
+        exp_sums = [keep.tile([P, BATCH], F32, name=f"exp_sums{b}") for b in batches]
+        log_sums = [keep.tile([P, BATCH], F32, name=f"log_sums{b}") for b in batches]
+        shifts = [keep.tile([P, BATCH], F32, name=f"shifts{b}") for b in batches]
+
+        def scores(i):
+            b, j = divmod(i, BATCH)
+            rows = slice(P * i, P * (i + 1))
+            negated[i] = stage.tile([P, V], F32, name="negated", tag="negated", bufs=6)
+            for c in range(V_GROUPS):
+                cols = slice(GROUP * c, GROUP * (c + 1))
+                acc = sums_psum.tile([P, GROUP], F32, name="acc", tag="acc")
+                for group in range(J_GROUPS):
+                    nc.tensor.matmul_mx(
+                        out=acc[:],
+                        lhsT=context_codes[:, group, rows].bitcast(FP8X4),
+                        lhsT_scale=context_scales[:, group, rows],
+                        rhs=label_codes[:, group, cols].bitcast(FP8X4),
+                        rhs_scale=label_scales[:, group, cols],
+                        start=(group == 0),
+                        stop=(group == J_GROUPS - 1),
+                    )
+                nc.vector.tensor_scalar(
+                    out=negated[i][:, cols],
+                    in0=acc[:],
+                    scalar1=-SCORE_SCALE,
+                    scalar2=None,
+                    op0=ALU.mult,
+                    op1=ALU.min,
+                    accum_out=minima[b][:, j, c : c + 1],
+                )
+            nc.vector.tensor_reduce(out=minus_max[b][:, j : j + 1], in_=minima[b][:, j, :], op=ALU.min, axis=AX.X)
+
+        def exponentials(i):
+            b, j = divmod(i, BATCH)
+            unread = stage.tile([P, V], BF16, name="unread", tag="unread", bufs=1)
+            nc.scalar.activation(
+                out=unread[:],
+                in_=negated[i][:],
+                func=ACT.Exp,
+                bias=minus_max[b][:, j : j + 1],
+                scale=-1.0,
+                accum_out=exp_sums[b][:, j : j + 1],
+            )
+
+        def take_logs(b):
+            nc.scalar.activation(out=log_sums[b][:], in_=exp_sums[b][:], func=ACT.Ln, scale=1.0 / V)
+
+        def make_shifts(b):
+            nc.vector.tensor_tensor(out=shifts[b][:], in0=minus_max[b][:], in1=log_sums[b][:], op=ALU.subtract)
+
+        def shift_of(i):
+            b, j = divmod(i, BATCH)
+            return shifts[b][:, j : j + 1]
+
+        def round_result(i):
+            rounded[i] = stage.tile([P, V], BF16, name="rounded", tag="rounded", bufs=3, align_bytes=64)
+            nc.vector.tensor_scalar(
+                out=rounded[i][:], in0=negated[i][:], scalar1=-1.0, scalar2=shift_of(i), op0=ALU.mult, op1=ALU.add
+            )
+
+        def store_result(i, on_scalar):
+            result = stage.tile([P, V], F32, name="result", tag="result", bufs=3)
+            if on_scalar:
+                nc.scalar.activation(out=result[:], in_=negated[i][:], func=ACT.Identity, bias=shift_of(i), scale=-1.0)
+            else:
+                nc.vector.tensor_scalar(
+                    out=result[:], in0=negated[i][:], scalar1=-1.0, scalar2=shift_of(i), op0=ALU.mult, op1=ALU.add
+                )
+            nc.sync.dma_start(out=out[P * i : P * (i + 1), :], in_=result[:])
+
+        def turn_result(i):
+            pair, row0 = i // 2, P * (i % 2)
+            if i % 2 == 0:
+                result_grouped[pair] = stage.tile(
+                    [P, V_GROUPS, 2 * P, SLOTS], BF16, name="result_grouped", tag="result_grouped", bufs=2, align_bytes=64
+                )
+                result_codes[pair] = stage.tile([P, V_GROUPS, 2 * P], I32, name="result_codes", tag="result_codes", bufs=2, align_bytes=64)
+            for g0, g1 in ((0, 2), (2, 3)):
+                turned = turn_psum.tile([P, 2, 2, P], F32, name="turned_result", tag="turn")
+                for g in range(g0, g1):
+                    turn_words(rounded[i][:].bitcast(F32), turned[:, g - g0], g)
+                nc.scalar.copy(
+                    out=result_grouped[pair][:, g0:g1, row0 : row0 + P, :]
+                    .rearrange("p g r t -> p g (r t)")
+                    .bitcast(F32)
+                    .rearrange("p g (r u) -> p g r u", u=2),
+                    in_=turned[:, 0 : g1 - g0].rearrange("p g u r -> p g r u"),
                 )
 
-        FINAL_ON = "SSSSSVSV"
-        units = [
-            label_unit(0, 256, 0), label_unit(256, 256, 0), label_unit(512, 512, 0), label_unit(0, 512, 1), label_unit(512, 512, 1),
-            context_unit(0, 512, 0), context_unit(0, 512, 1), label_unit(1024, 512, 0), label_unit(1024, 512, 1),
-            context_unit(512, 512, 0), context_unit(512, 512, 1),
-        ]
-        permute_scales(0)
-        permute_words(u_codes, u_raw, 0)
-        project(units[0])
-        permute_scales(1)
-        project(units[1])
-        gain(units[0])
-        permute_words(u_codes, u_raw, 1)
-        project(units[2])
-        gain(units[1])
-        quant(units[0])
-        quant(units[1])
-        permute_words(vp_codes, vp_raw, 0)
-        project(units[3])
-        h_turn(0)
-        h_turn(1)
-        gain(units[2], 0, 2)
-        permute_words(vp_codes, vp_raw, 1)
-        gain(units[2], 1, 2)
-        project(units[4])
-        h_turn(2)
-        h_turn(3)
-        gain(units[3], 0, 2)
-        quant(units[2])
-        gain(units[3], 1, 2)
-        h_quant(0, 0)
-        h_quant(0, 1)
-        project(units[5])
-        gain(units[4], 0, 2)
-        quant(units[3])
-        gain(units[4], 1, 2)
-        project(units[6])
-        h_turn(4)
-        h_turn(5)
-        gain(units[5], 0, 2)
-        quant(units[4])
-        gain(units[5], 1, 2)
-        project(units[7])
-        h_turn(6)
-        h_turn(7)
-        gain(units[6], 0, 2)
-        quant(units[5])
-        gain(units[6], 1, 2)
-        project(units[8])
-        gain(units[7], 0, 2)
-        quant(units[6])
-        h_quant(1, 0)
-        h_quant(1, 1)
-        gain(units[7], 1, 2)
-        project(units[9])
-        gain(units[8], 0, 2)
-        quant(units[7])
-        gain(units[8], 1, 2)
-        project(units[10])
-        gain(units[9], 0, 2)
-        quant(units[8])
-        scores(0)
-        exps(0)
-        scores(1)
-        exps(1)
-        gain(units[9], 1, 2)
-        logs(0)
-        scores(2)
-        exps(2)
-        logs(1)
-        quant(units[9])
-        final_b(0)
-        final_f(0)
-        gain(units[10], 0, 2)
-        scores(3)
-        turn(0)
-        final_f(1)
-        logs(2)
-        exps(3)
-        final_b(1)
-        gain(units[10], 1, 2)
-        plane_quant(0)
-        logs(3)
-        quant(units[10])
-        turn(1)
-        final_b(2)
-        final_f(2)
-        for i in range(4, NT):
+        def quantise_result(i, tiles):
+            pair, row0, width = i // 2, P * (i % 2), P * tiles
+            for g in range(V_GROUPS):
+                nc.vector.quantize_mx(
+                    out=result_codes[pair][:, g, row0 : row0 + width].bitcast(FP8X4),
+                    scales=result_scales[:, g, P * i : P * i + width],
+                    in_=result_grouped[pair][:, g, row0 : row0 + width, :].rearrange("p r t -> p (r t)"),
+                )
+            nc.sync.dma_start(
+                out=out_words.rearrange("g p m t -> p g (m t)")[:, :, SLOTS * P * i : SLOTS * (P * i + width)].bitcast(I32),
+                in_=result_codes[pair][:, :, row0 : row0 + width],
+            )
+
+        def store_result_scales(half):
+            cols = slice(512 * half, 512 * (half + 1))
+            for q in range(4):
+                nc.sync.dma_start(
+                    out=out_scales.rearrange("g q m -> q g m")[4 * q : 4 * q + 4, :, cols].bitcast(I32),
+                    in_=result_scales[32 * q : 32 * q + 4, :, cols].bitcast(I32),
+                )
+
+        spread_vectors()
+        slot_scales("u")
+        for g in range(D_GROUPS):
+            slot_words("u", g, 0, 512)
+        project(label_blocks[0])
+        project(label_blocks[1])
+        apply_gain(label_blocks[0])
+        for g in range(D_GROUPS):
+            slot_words("u", g, 512, 1024)
+        apply_gain(label_blocks[1])
+        slot_scales("vp")
+        quantise(label_blocks[0])
+        slot_words("vp", 0, 0, 1024)
+        quantise(label_blocks[1])
+        slot_words("vp", 1, 0, 1024)
+
+        blocks = label_blocks[2:] + context_blocks[:2]
+        h_turns_after = {1: (0, 1), 2: (2, 3), 4: (4, 5), 5: (6, 7)}
+        h_half_after = {3: 0, 5: 1}
+        for k, block in enumerate(blocks):
+            project(block)
+            for i in h_turns_after.get(k, ()):
+                turn_h(i)
+            if k in h_half_after:
+                quantise_h(h_half_after[k])
+            apply_gain(block)
+            if k > 0:
+                quantise(blocks[k - 1])
+        project(context_blocks[2])
+        quantise(context_blocks[1])
+        apply_gain(context_blocks[2])
+        project(context_blocks[3])
+
+        for i in range(4):
             scores(i)
-            turn(i - 2)
-            exps(i)
-            plane_quant(i - 3)
-            final_b(i - 1)
-            final_f(i - 1)
-            logs(i)
-            if i == 6:
-                store_scales(0, 512)
-        final_b(NT - 1)
-        turn(NT - 2)
-        final_f(NT - 1)
-        plane_quant(NT - 3)
-        turn(NT - 1)
-        plane_quant(NT - 2)
-        plane_quant(NT - 1)
-        store_scales(512, 1024)
+        apply_gain(context_blocks[3])
+        for i in range(4):
+            exponentials(i)
+        quantise(context_blocks[2])
+        quantise(context_blocks[3])
+        take_logs(0)
+        make_shifts(0)
+
+        round_result(0)
+        scores(4)
+        store_result(3, on_scalar=True)
+        store_result(0, on_scalar=True)
+        turn_result(0)
+        exponentials(4)
+        round_result(1)
+        store_result(1, on_scalar=False)
+        scores(5)
+        scores(6)
+        turn_result(1)
+        exponentials(5)
+        scores(7)
+        exponentials(6)
+        round_result(2)
+        store_result(2, on_scalar=False)
+        exponentials(7)
+        take_logs(1)
+        quantise_result(0, tiles=2)
+        turn_result(2)
+        round_result(3)
+
+        make_shifts(1)
+        store_result(4, on_scalar=False)
+        round_result(4)
+        store_result(5, on_scalar=False)
+        turn_result(3)
+        round_result(5)
+        quantise_result(2, tiles=2)
+        store_result_scales(0)
+        round_result(6)
+        store_result(6, on_scalar=True)
+        store_result(7, on_scalar=False)
+        for i in (4, 5, 6):
+            turn_result(i)
+        round_result(7)
+        quantise_result(4, tiles=2)
+        turn_result(7)
+        quantise_result(6, tiles=1)
+        quantise_result(7, tiles=1)
+        store_result_scales(1)

import math
from contextlib import ExitStack

import concourse.mybir as mybir
from concourse.masks import make_identity

F32 = mybir.dt.float32
BF16 = mybir.dt.bfloat16
I32 = mybir.dt.int32
U8 = mybir.dt.uint8
FP8X4 = mybir.dt.float8_e4m3fn_x4
ACT = mybir.ActivationFunctionType
ALU = mybir.AluOpType
AX = mybir.AxisListType

P = 128
N, D, J, V = 1024, 1024, 1024, 1536
SLOTS = 4
GROUP = P * SLOTS
D_GROUPS, J_GROUPS, V_GROUPS = D // GROUP, J // GROUP, V // GROUP
RUN = 8
TOKEN_TILES = N // P
BATCH = 4
SCORE_SCALE = 2.0 / math.sqrt(J)
LABEL_BIAS, CONTEXT_BIAS, LABEL_GAIN, CONTEXT_GAIN = 0, 2, 4, 6

FLOPS = 2 * (V * D * J + N * D * J + N * J * V)


def tile_jointinputoutputembeddingtiedhead_x2_kernel(
    tc, h, emb_words, emb_scales, u_words, u_scales, vp_words, vp_scales, bj, gu, gv, out, out_words, out_scales
):
    nc = tc.nc
    with ExitStack() as stack:
        keep = stack.enter_context(tc.tile_pool(name="keep", bufs=1))
        stage = stack.enter_context(tc.tile_pool(name="stage", bufs=3))
        sums_psum = stack.enter_context(tc.psum_pool(name="sums_psum", bufs=6))
        turn_psum = stack.enter_context(tc.psum_pool(name="turn_psum", bufs=2))
        stack.enter_context(tc.manual_schedule())

        vector_rows = keep.tile([P, GROUP], BF16, name="vector_rows")
        nc.gpsimd.memset(vector_rows[:], 0.0)

        arrived_scales = {}
        for name, width in (("u", J), ("emb", V), ("vp", J)):
            arrived_scales[name] = keep.tile([P, width], U8, name=f"{name}_arrived_scales", align_bytes=64)
            nc.vector.memset(arrived_scales[name][:].bitcast(I32), 0)

        arrived_words = {}
        for name in ("u", "vp"):
            arrived_words[name] = stage.tile([P, D_GROUPS, J], I32, name=f"{name}_arrived", tag="tanh", bufs=5, align_bytes=64)
        emb_codes = keep.tile([P, D_GROUPS, V], I32, name="emb_codes", align_bytes=64)
        h_rows = [keep.tile([P, D], BF16, name=f"h_rows{i}", align_bytes=64) for i in range(TOKEN_TILES)]

        nc.scalar.dma_start(out=vector_rows[0:4, :], in_=bj.rearrange("v (g x) -> (v g) x", g=J_GROUPS))
        nc.scalar.dma_start(out=vector_rows[4:6, :], in_=gu.rearrange("(g x) -> g x", g=J_GROUPS))
        nc.scalar.dma_start(out=vector_rows[6:8, :], in_=gv.rearrange("(g x) -> g x", g=J_GROUPS))

        def load_scales(name, scales):
            for q in range(4):
                nc.sync.dma_start(
                    out=arrived_scales[name][32 * q : 32 * q + 8, :].bitcast(I32),
                    in_=scales[:, 4 * q : 4 * q + 4, :].bitcast(I32),
                )

        def load_words(tile, words, c0, c1):
            for g in range(D_GROUPS):
                nc.sync.dma_start(
                    out=tile[:, g, c0:c1],
                    in_=words[g].rearrange("p n t -> p (n t)")[:, SLOTS * c0 : SLOTS * c1].bitcast(I32),
                )

        def load_h(i):
            nc.sync.dma_start(out=h_rows[i][:], in_=h[P * i : P * (i + 1), :])

        load_scales("u", u_scales)
        load_scales("emb", emb_scales)
        load_words(arrived_words["u"], u_words, 0, 512)
        load_words(emb_codes, emb_words, 0, 256)
        load_words(emb_codes, emb_words, 256, 512)
        load_words(emb_codes, emb_words, 512, 1024)
        load_words(arrived_words["u"], u_words, 512, 1024)
        load_scales("vp", vp_scales)
        load_words(arrived_words["vp"], vp_words, 0, 1024)
        for i in range(4):
            load_h(i)
        load_words(emb_codes, emb_words, 1024, 1536)
        for i in range(4, TOKEN_TILES):
            load_h(i)

        identity = keep.tile([P, P], F32, name="identity")
        make_identity(nc, identity[:])

        slotted_rows = keep.tile([P, GROUP], F32, name="slotted_rows")
        columns = keep.tile([P, 8, SLOTS], F32, name="columns")

        def spread_vectors():
            nc.vector.tensor_copy(
                out=slotted_rows[:].rearrange("p (t b i) -> p t b i", t=SLOTS, i=RUN),
                in_=vector_rows[:].rearrange("p (b t i) -> p t b i", t=SLOTS, i=RUN),
            )
            turned = turn_psum.tile([P, SLOTS, P], F32, name="turned_rows", tag="turn")
            for t in range(SLOTS):
                nc.tensor.transpose(turned[:, t, :], slotted_rows[:, P * t : P * (t + 1)], identity[:])
            nc.scalar.copy(out=columns[:], in_=turned[:, :, 0:8].rearrange("p t r -> p r t"))

        weight_codes = {
            name: keep.tile([P, D_GROUPS, SLOTS, J // SLOTS], I32, name=f"{name}_codes", align_bytes=64) for name in ("u", "vp")
        }
        weight_scales = {name: keep.tile([P, SLOTS, J // SLOTS], U8, name=f"{name}_scales", align_bytes=64) for name in ("u", "vp")}

        def slot_words(name, g, c0, c1):
            nc.vector.tensor_copy(
                out=weight_codes[name][:, g, :, c0 // SLOTS : c1 // SLOTS].rearrange("p t (b i) -> p t b i", i=RUN),
                in_=arrived_words[name][:, g, c0:c1].rearrange("p (b t i) -> p t b i", t=SLOTS, i=RUN),
            )

        def slot_scales(name):
            nc.vector.tensor_copy(
                out=weight_scales[name][:].rearrange("p t m -> p (t m)").bitcast(I32).rearrange("p (t b i) -> p t b i", t=SLOTS, i=2),
                in_=arrived_scales[name][:].bitcast(I32).rearrange("p (b t i) -> p t b i", t=SLOTS, i=2),
            )

        h_codes = keep.tile([P, D_GROUPS, N], I32, name="h_codes", align_bytes=64)
        h_scales = keep.tile([P, D_GROUPS, N], U8, name="h_scales", align_bytes=64)
        label_codes = keep.tile([P, J_GROUPS, V], I32, name="label_codes", align_bytes=64)
        label_scales = keep.tile([P, J_GROUPS, V], U8, name="label_scales", align_bytes=64)
        context_codes = keep.tile([P, J_GROUPS, N], I32, name="context_codes", align_bytes=64)
        context_scales = keep.tile([P, J_GROUPS, N], U8, name="context_scales", align_bytes=64)
        result_scales = keep.tile([P, V_GROUPS, N], U8, name="result_scales", align_bytes=64)

        h_grouped = {}

        def turn_words(words, turned, group):
            for u in range(2):
                nc.tensor.transpose(turned[:, u, :], words[:, 256 * group + u : 256 * (group + 1) : 2], identity[:])

        def turn_h(i):
            half, row0 = i // 4, P * (i % 4)
            if i % 4 == 0:
                h_grouped[half] = stage.tile([P, D_GROUPS, 512, SLOTS], BF16, name="h_grouped", tag="h_grouped", bufs=1, align_bytes=64)
            turned = turn_psum.tile([P, D_GROUPS, 2, P], F32, name="turned_h", tag="turn")
            for g in range(D_GROUPS):
                turn_words(h_rows[i][:].bitcast(F32), turned[:, g], g)
            nc.scalar.copy(
                out=h_grouped[half][:, :, row0 : row0 + P, :]
                .rearrange("p g r t -> p g (r t)")
                .bitcast(F32)
                .rearrange("p g (r u) -> p g r u", u=2),
                in_=turned[:].rearrange("p g u r -> p g r u"),
            )

        def quantise_h(half):
            cols = slice(512 * half, 512 * (half + 1))
            for g in range(D_GROUPS):
                nc.vector.quantize_mx(
                    out=h_codes[:, g, cols].bitcast(FP8X4),
                    scales=h_scales[:, g, cols],
                    in_=h_grouped[half][:, g].rearrange("p r t -> p (r t)"),
                )

        label_blocks = [
            ("label", 0, 256, 0),
            ("label", 256, 256, 0),
            ("label", 512, 512, 0),
            ("label", 0, 512, 1),
            ("label", 512, 512, 1),
            ("label", 1024, 512, 0),
            ("label", 1024, 512, 1),
        ]
        context_blocks = [("context", 512 * half, 512, group) for half in range(2) for group in range(J_GROUPS)]
        gain_on_scalar = context_blocks[2]

        tanh_tiles, scaled_tiles, grouped_tiles = {}, {}, {}

        def project(block):
            side, c0, width, group = block
            cols = slice(c0, c0 + width)
            if side == "label":
                weight, bias, gain, codes, scales = "u", LABEL_BIAS, LABEL_GAIN, emb_codes, None
            else:
                weight, bias, gain, codes, scales = "vp", CONTEXT_BIAS, CONTEXT_GAIN, h_codes, h_scales
            tanh_tiles[block] = stage.tile([P, SLOTS, width], F32, name="tanh", tag="tanh", bufs=5, align_bytes=64)
            if block == gain_on_scalar:
                scaled_tiles[block] = stage.tile([P, SLOTS, width], BF16, name="scaled", tag="rounded", bufs=3, align_bytes=64)
            for t in range(SLOTS):
                acc = sums_psum.tile([P, width], F32, name="acc", tag="acc")
                for g in range(D_GROUPS):
                    nc.tensor.matmul_mx(
                        out=acc[:],
                        lhsT=weight_codes[weight][:, g, t, P * group : P * (group + 1)].bitcast(FP8X4),
                        lhsT_scale=weight_scales[weight][4 * g :, t, P * group : P * (group + 1)],
                        rhs=codes[:, g, cols].bitcast(FP8X4),
                        rhs_scale=arrived_scales["emb"][4 * g :, cols] if scales is None else scales[:, g, cols],
                        start=(g == 0),
                        stop=(g == D_GROUPS - 1),
                    )
                nc.scalar.activation(
                    out=tanh_tiles[block][:, t, :], in_=acc[:], func=ACT.Tanh, bias=columns[:, bias + group, t : t + 1], scale=1.0
                )
                if block == gain_on_scalar:
                    nc.scalar.activation(
                        out=scaled_tiles[block][:, t, :],
                        in_=tanh_tiles[block][:, t, :],
                        func=ACT.Copy,
                        scale=columns[:, gain + group, t : t + 1],
                    )

        def apply_gain(block):
            side, c0, width, group = block
            gain = LABEL_GAIN if side == "label" else CONTEXT_GAIN
            grouped = stage.tile([P, width, SLOTS], BF16, name="grouped", tag="grouped", align_bytes=64)
            grouped_tiles[block] = grouped
            if block == gain_on_scalar:
                nc.vector.tensor_copy(
                    out=grouped[:].rearrange("p (c i) t -> p c t i", i=4),
                    in_=scaled_tiles[block][:].rearrange("p t (c i) -> p c t i", i=4),
                )
                return
            nc.vector.tensor_tensor(
                out=grouped[:].rearrange("p (c i) t -> p c t i", i=2),
                in0=tanh_tiles[block][:].rearrange("p t (c i) -> p c t i", i=2),
                in1=columns[:, gain + group, :].unsqueeze(1).unsqueeze(3).to_broadcast([P, width // 2, SLOTS, 2]),
                op=ALU.mult,
            )

        def quantise(block):
            side, c0, width, group = block
            codes, scales = (label_codes, label_scales) if side == "label" else (context_codes, context_scales)
            nc.vector.quantize_mx(
                out=codes[:, group, c0 : c0 + width].bitcast(FP8X4),
                scales=scales[:, group, c0 : c0 + width],
                in_=grouped_tiles[block][:].rearrange("p c t -> p (c t)"),
            )

        negated, rounded, result_grouped, result_codes = {}, {}, {}, {}
        batches = range(TOKEN_TILES // BATCH)
        minima = [keep.tile([P, BATCH, V_GROUPS], F32, name=f"minima{b}") for b in batches]
        minus_max = [keep.tile([P, BATCH], F32, name=f"minus_max{b}") for b in batches]
        exp_sums = [keep.tile([P, BATCH], F32, name=f"exp_sums{b}") for b in batches]
        log_sums = [keep.tile([P, BATCH], F32, name=f"log_sums{b}") for b in batches]
        shifts = [keep.tile([P, BATCH], F32, name=f"shifts{b}") for b in batches]

        def scores(i):
            b, j = divmod(i, BATCH)
            rows = slice(P * i, P * (i + 1))
            negated[i] = stage.tile([P, V], F32, name="negated", tag="negated", bufs=6)
            for c in range(V_GROUPS):
                cols = slice(GROUP * c, GROUP * (c + 1))
                acc = sums_psum.tile([P, GROUP], F32, name="acc", tag="acc")
                for group in range(J_GROUPS):
                    nc.tensor.matmul_mx(
                        out=acc[:],
                        lhsT=context_codes[:, group, rows].bitcast(FP8X4),
                        lhsT_scale=context_scales[:, group, rows],
                        rhs=label_codes[:, group, cols].bitcast(FP8X4),
                        rhs_scale=label_scales[:, group, cols],
                        start=(group == 0),
                        stop=(group == J_GROUPS - 1),
                    )
                nc.vector.tensor_scalar(
                    out=negated[i][:, cols],
                    in0=acc[:],
                    scalar1=-SCORE_SCALE,
                    scalar2=None,
                    op0=ALU.mult,
                    op1=ALU.min,
                    accum_out=minima[b][:, j, c : c + 1],
                )
            nc.vector.tensor_reduce(out=minus_max[b][:, j : j + 1], in_=minima[b][:, j, :], op=ALU.min, axis=AX.X)

        def exponentials(i):
            b, j = divmod(i, BATCH)
            unread = stage.tile([P, V], BF16, name="unread", tag="unread", bufs=1)
            nc.scalar.activation(
                out=unread[:],
                in_=negated[i][:],
                func=ACT.Exp,
                bias=minus_max[b][:, j : j + 1],
                scale=-1.0,
                accum_out=exp_sums[b][:, j : j + 1],
            )

        def take_logs(b):
            nc.scalar.activation(out=log_sums[b][:], in_=exp_sums[b][:], func=ACT.Ln, scale=1.0 / V)

        def make_shifts(b):
            nc.vector.tensor_tensor(out=shifts[b][:], in0=minus_max[b][:], in1=log_sums[b][:], op=ALU.subtract)

        def shift_of(i):
            b, j = divmod(i, BATCH)
            return shifts[b][:, j : j + 1]

        def round_result(i):
            rounded[i] = stage.tile([P, V], BF16, name="rounded", tag="rounded", bufs=3, align_bytes=64)
            nc.vector.tensor_scalar(
                out=rounded[i][:], in0=negated[i][:], scalar1=-1.0, scalar2=shift_of(i), op0=ALU.mult, op1=ALU.add
            )

        def store_result(i, on_scalar):
            result = stage.tile([P, V], F32, name="result", tag="result", bufs=3)
            if on_scalar:
                nc.scalar.activation(out=result[:], in_=negated[i][:], func=ACT.Identity, bias=shift_of(i), scale=-1.0)
            else:
                nc.vector.tensor_scalar(
                    out=result[:], in0=negated[i][:], scalar1=-1.0, scalar2=shift_of(i), op0=ALU.mult, op1=ALU.add
                )
            nc.sync.dma_start(out=out[P * i : P * (i + 1), :], in_=result[:])

        def turn_result(i):
            pair, row0 = i // 2, P * (i % 2)
            if i % 2 == 0:
                result_grouped[pair] = stage.tile(
                    [P, V_GROUPS, 2 * P, SLOTS], BF16, name="result_grouped", tag="result_grouped", bufs=2, align_bytes=64
                )
                result_codes[pair] = stage.tile([P, V_GROUPS, 2 * P], I32, name="result_codes", tag="result_codes", bufs=2, align_bytes=64)
            for g0, g1 in ((0, 2), (2, 3)):
                turned = turn_psum.tile([P, 2, 2, P], F32, name="turned_result", tag="turn")
                for g in range(g0, g1):
                    turn_words(rounded[i][:].bitcast(F32), turned[:, g - g0], g)
                nc.scalar.copy(
                    out=result_grouped[pair][:, g0:g1, row0 : row0 + P, :]
                    .rearrange("p g r t -> p g (r t)")
                    .bitcast(F32)
                    .rearrange("p g (r u) -> p g r u", u=2),
                    in_=turned[:, 0 : g1 - g0].rearrange("p g u r -> p g r u"),
                )

        def quantise_result(i, tiles):
            pair, row0, width = i // 2, P * (i % 2), P * tiles
            for g in range(V_GROUPS):
                nc.vector.quantize_mx(
                    out=result_codes[pair][:, g, row0 : row0 + width].bitcast(FP8X4),
                    scales=result_scales[:, g, P * i : P * i + width],
                    in_=result_grouped[pair][:, g, row0 : row0 + width, :].rearrange("p r t -> p (r t)"),
                )
            nc.sync.dma_start(
                out=out_words.rearrange("g p m t -> p g (m t)")[:, :, SLOTS * P * i : SLOTS * (P * i + width)].bitcast(I32),
                in_=result_codes[pair][:, :, row0 : row0 + width],
            )

        def store_result_scales(half):
            cols = slice(512 * half, 512 * (half + 1))
            for q in range(4):
                nc.sync.dma_start(
                    out=out_scales.rearrange("g q m -> q g m")[4 * q : 4 * q + 4, :, cols].bitcast(I32),
                    in_=result_scales[32 * q : 32 * q + 4, :, cols].bitcast(I32),
                )

        spread_vectors()
        slot_scales("u")
        for g in range(D_GROUPS):
            slot_words("u", g, 0, 512)
        project(label_blocks[0])
        project(label_blocks[1])
        apply_gain(label_blocks[0])
        for g in range(D_GROUPS):
            slot_words("u", g, 512, 1024)
        apply_gain(label_blocks[1])
        slot_scales("vp")
        quantise(label_blocks[0])
        slot_words("vp", 0, 0, 1024)
        quantise(label_blocks[1])
        slot_words("vp", 1, 0, 1024)

        blocks = label_blocks[2:] + context_blocks[:2]
        h_turns_after = {1: (0, 1), 2: (2, 3), 4: (4, 5), 5: (6, 7)}
        h_half_after = {3: 0, 5: 1}
        for k, block in enumerate(blocks):
            project(block)
            for i in h_turns_after.get(k, ()):
                turn_h(i)
            if k in h_half_after:
                quantise_h(h_half_after[k])
            apply_gain(block)
            if k > 0:
                quantise(blocks[k - 1])
        project(context_blocks[2])
        quantise(context_blocks[1])
        apply_gain(context_blocks[2])
        project(context_blocks[3])

        for i in range(4):
            scores(i)
        apply_gain(context_blocks[3])
        for i in range(4):
            exponentials(i)
        quantise(context_blocks[2])
        quantise(context_blocks[3])
        take_logs(0)
        make_shifts(0)

        round_result(0)
        scores(4)
        store_result(3, on_scalar=True)
        store_result(0, on_scalar=True)
        turn_result(0)
        exponentials(4)
        round_result(1)
        store_result(1, on_scalar=False)
        scores(5)
        scores(6)
        turn_result(1)
        exponentials(5)
        scores(7)
        exponentials(6)
        round_result(2)
        store_result(2, on_scalar=False)
        exponentials(7)
        take_logs(1)
        quantise_result(0, tiles=2)
        turn_result(2)
        round_result(3)

        make_shifts(1)
        store_result(4, on_scalar=False)
        round_result(4)
        store_result(5, on_scalar=False)
        turn_result(3)
        round_result(5)
        quantise_result(2, tiles=2)
        store_result_scales(0)
        round_result(6)
        store_result(6, on_scalar=True)
        store_result(7, on_scalar=False)
        for i in (4, 5, 6):
            turn_result(i)
        round_result(7)
        quantise_result(4, tiles=2)
        turn_result(7)
        quantise_result(6, tiles=1)
        quantise_result(7, tiles=1)
        store_result_scales(1)
